import numpy as np
import ml_dtypes


def mxq(x, axis, fmt="e4m3"):
    dtype, down = {"e4m3": (ml_dtypes.float8_e4m3fn, 7), "e5m2": (ml_dtypes.float8_e5m2, 14)}[fmt]
    v = np.moveaxis(np.asarray(x, np.float32).astype(ml_dtypes.bfloat16).astype(np.float64), axis, -1)
    blocks = v.reshape(v.shape[:-1] + (-1, 32))
    amax = np.abs(blocks).max(-1, keepdims=True)
    byte = np.maximum(np.where(amax > 0, np.frexp(amax)[1] - 1 + 127, 0) - down, 1)
    scale = np.exp2(byte - 127.0)
    codes = (blocks / scale).astype(np.float32).astype(dtype).astype(np.float64)
    return np.moveaxis((codes * scale).reshape(v.shape), -1, axis)


WIDE = False


def mx_kscale(k):
    if not WIDE:
        return np.ones(k)
    levels = np.array([10, -10, 5, -5, 0])
    if k % 512:
        return np.exp2(np.random.permutation(np.resize(levels, k // 32))).repeat(32)
    a = np.empty((k // 512, 16))
    for p in range(k // 512):
        a[p, :8] = np.random.permutation(np.resize(levels, 8))
        for g in range(8):
            far = levels[np.abs(levels - a[p, g]) >= 10]
            a[p, g + 8] = far[np.random.randint(len(far))]
    return np.exp2(a.ravel()).repeat(32)


def f64(x):
    return np.asarray(x).astype(np.float64)


def striped(idx):
    return np.tile(np.asarray(idx).reshape(-1, 16).T, (8, 1)).astype(np.uint16)


def unstriped(offs):
    return offs[:16].T.reshape(-1).astype(np.int64)


E2M1 = np.array([0.0, 0.5, 1.0, 1.5, 2.0, 3.0, 4.0, 6.0, -0.0, -0.5, -1.0, -1.5, -2.0, -3.0, -4.0, -6.0])


def pack_weight(w, fmt):
    k, n = w.shape
    w = f64(np.asarray(w, np.float32).astype(ml_dtypes.bfloat16)).reshape(k // 32, 32, n)
    amax = np.abs(w).max(1)
    if fmt == "e4m3":
        byte = np.frexp(amax)[1] - 1 + 127 - 7
    else:
        mant, ex = np.frexp(amax / 6.0)
        byte = np.where(mant > 0.5, ex, ex - 1) + 127
    byte = np.clip(np.where(amax > 0, byte, 1), 1, 254)
    scaled = (w * np.exp2(127.0 - byte)[:, None, :]).reshape(k, n).astype(np.float32)
    by_word = np.ascontiguousarray(scaled.reshape(k // 512, 128, 4, n).transpose(0, 1, 3, 2))
    if fmt == "e4m3":
        words = by_word.astype(ml_dtypes.float8_e4m3fn).view(np.uint8)
    else:
        c = by_word.astype(ml_dtypes.float4_e2m1fn).view(np.uint8) & 0xF
        words = (c[..., 0::2] | (c[..., 1::2] << 4)).reshape(k // 512, 128, 2 * n)
    return np.ascontiguousarray(words), np.ascontiguousarray(byte.astype(np.uint8).reshape(k // 512, 16, n))


def unpack_weight(words, scales, fmt):
    g, _, n = scales.shape
    words = np.ascontiguousarray(words).reshape(g, 128, n, -1)
    if fmt == "e4m3":
        vals = words.view(ml_dtypes.float8_e4m3fn).astype(np.float64)
    else:
        nib = np.empty((g, 128, n, 4), np.uint8)
        nib[..., 0::2] = words & 0xF
        nib[..., 1::2] = words >> 4
        vals = E2M1[nib]
    vals = vals * np.repeat(np.exp2(scales.astype(np.float64) - 127.0), 8, axis=1)[..., None]
    return vals.transpose(0, 1, 3, 2).reshape(g * 512, n)


D, T, I, Q, E, G = 512, 2048, 512, 128, 512, 64


def setup_inputs():
    n = np.random.standard_normal
    idx = np.random.permutation(T)[:I]
    fd = mx_kscale(D)
    fi = mx_kscale(I)
    ti = np.ones(T)
    ti[idx] = fi
    keysp = pack_weight(n((D, T)) / fd[:, None], "e4m3")
    return {
        "query": (n((D, Q)) * 0.7 / np.sqrt(D) * fd[:, None]).astype(np.float32),
        "query2": (n((D, Q)) * 0.7 / np.sqrt(D) * fd[:, None]).astype(np.float32),
        "keys_words": keysp[0],
        "keys_scales": keysp[1],
        "xmark": np.tile(np.random.uniform(-1.0, 1.0, T), (128, 1)).astype(np.float32),
        "ymark": np.tile(np.random.uniform(-1.0, 1.0, T), (128, 1)).astype(np.float32),
        "lam": (np.random.uniform(0.5, 1.2, (Q, 1))).astype(np.float32),
        "os": (np.random.uniform(4.0, 16.0, (1, I)) * fi).astype(np.float32),
        "vals": (n((E, T)) / ti).astype(np.float32),
        "before": (n((Q, E))).astype(np.float32),
        "hold": (np.random.uniform(0.1, 0.6, (Q, 1))).astype(np.float32),
        "offs": striped(idx),
    }


def reference(query, query2, keys_words, keys_scales, xmark, ymark, lam, os, vals, before, hold, offs):
    idx = unstriped(offs)
    keysu = unpack_weight(keys_words, keys_scales, "e4m3")
    queryq = mxq(f64(query), 0, "e4m3")
    keysidxg = keysu[:, idx]
    a = queryq.T @ keysidxg
    query2q = mxq(f64(query2), 0, "e4m3")
    b = query2q.T @ keysidxg
    dx = a - f64(xmark)[:1][:, idx]
    dy = b - f64(ymark)[:1][:, idx]
    s = (np.square(dx) + np.square(dy)) * f64(lam) * (-1.0)
    p = np.exp(s)
    pg = p.reshape(Q, G, I // G).sum(axis=2)
    z0 = np.sum(pg, axis=1, keepdims=True)
    k0 = 1.0 / (z0 - pg)
    kr = np.repeat(k0, I // G, axis=1)
    w = p * kr
    wo1 = w * f64(os)
    wt1 = wo1.T
    vt1 = f64(vals)[:, idx].T
    wt1q = mxq(wt1, 0, "e4m3")
    vt1q = mxq(vt1, 0, "e4m3")
    o = wt1q.T @ vt1q
    y = f64(before) * f64(hold) + o * (1.0 - f64(hold))
    return y

@@ -1,0 +1,229 @@
+from contextlib import ExitStack
+
+import concourse.mybir as mybir
+from concourse.masks import make_identity
+
+D, T, I, Q, E, G = 512, 2048, 512, 128, 512, 64
+P = 128
+PACK = 4
+FLOPS = 2 * D * Q * I * 2 + 2 * I * Q * E
+
+F32 = mybir.dt.float32
+BF16 = mybir.dt.bfloat16
+I32 = mybir.dt.int32
+U32 = mybir.dt.uint32
+U16 = mybir.dt.uint16
+U8 = mybir.dt.uint8
+X4 = mybir.dt.float8_e4m3fn_x4
+ALU = mybir.AluOpType
+ACT = mybir.ActivationFunctionType
+AX = mybir.AxisListType
+
+
+def tile_attend_maplace_outside_blend_kernel(
+    tc, query, query2, keys_words, keys_scales, xmark, ymark, lam, slot_factor, vals, before, hold, offs, out
+):
+    nc = tc.nc
+    with ExitStack() as ctx:
+        lists = ctx.enter_context(tc.tile_pool(name="lists", bufs=1))
+        sb = ctx.enter_context(tc.tile_pool(name="sb", bufs=1))
+        ps = ctx.enter_context(tc.psum_pool(name="ps", bufs=1))
+
+        def sbt(shape, dtype, name, tag=None):
+            return sb.tile(shape, dtype, name=name, tag=tag or name, align_bytes=64)
+
+        offsets = lists.tile([P, I // 16], U16, name="offsets")
+        nc.sync.dma_start(offsets[:], offs)
+
+        scale_win = sbt([P, T], U8, "scale_win", "slot0")
+        x_win = sbt([P, T], F32, "x_win", "slot1")
+        y_win = sbt([P, T], F32, "y_win", "slot2")
+        word_win = sbt([P, T], I32, "word_win", "slot3")
+        nc.vector.memset(scale_win[:].bitcast(I32), 0)
+        nc.vector.memset(x_win[:], 0.0)
+        nc.vector.memset(y_win[:], 0.0)
+
+        q_raw = [sbt([P, PACK, Q], F32, "q_raw%d" % c) for c in range(2)]
+        for raw, src in zip(q_raw, (query, query2)):
+            nc.scalar.dma_start(out=raw[:], in_=src.rearrange("(p t) q -> p t q", t=PACK))
+        nc.scalar.dma_start(out=word_win[:], in_=keys_words[0].rearrange("p n t -> p (n t)").bitcast(I32))
+
+        scale_rows = keys_scales[0].bitcast(I32).rearrange("(quad r) c -> r quad c", r=4)
+        for r in range(4):
+            nc.sync.dma_start(out=scale_win[r:P:32, :].bitcast(I32), in_=scale_rows[r])
+        nc.sync.dma_start(out=x_win[0:1, :], in_=xmark[0:1, :])
+        nc.sync.dma_start(out=y_win[0:1, :], in_=ymark[0:1, :])
+
+        ident = sbt([P, P], F32, "ident")
+        make_identity(nc, ident[:])
+        lam_col = sbt([P, 1], F32, "lam_col")
+        hold_col = sbt([P, 1], F32, "hold_col")
+        os_col = sbt([P, PACK], F32, "os_col")
+        nc.gpsimd.dma_start(out=lam_col[:], in_=lam)
+        nc.gpsimd.dma_start(out=hold_col[:], in_=hold)
+        nc.gpsimd.dma_start(out=os_col[:], in_=slot_factor.rearrange("o (p t) -> p (o t)", t=PACK))
+        neg_lam = sbt([P, 1], F32, "neg_lam")
+        keep_new = sbt([P, 1], F32, "keep_new")
+        nc.gpsimd.tensor_scalar(neg_lam[:], lam_col[:], -1.0, 0.0, ALU.mult, ALU.add)
+        nc.gpsimd.tensor_scalar(keep_new[:], hold_col[:], -1.0, 1.0, ALU.mult, ALU.add)
+
+        q_grp = sbt([P, 2, Q, PACK], BF16, "q_grp")
+        q_codes = sbt([P, 2 * Q], U32, "q_codes")
+        q_scales = sbt([P, 2 * Q], U8, "q_scales")
+        nc.vector.tensor_copy(
+            out=q_grp[:, 0].rearrange("p (c i) t -> p c t i", i=4),
+            in_=q_raw[0][:].rearrange("p t (c i) -> p c t i", i=4),
+        )
+        k_scales = sbt([P, I], U8, "k_scales")
+        nc.vector.tensor_copy(k_scales[:], scale_win[:].indirect(offsets[:]))
+        nc.vector.tensor_copy(
+            out=q_grp[:, 1].rearrange("p (c i) t -> p c t i", i=4),
+            in_=q_raw[1][:].rearrange("p t (c i) -> p c t i", i=4),
+        )
+        nc.vector.quantize_mx(
+            out=q_codes[:].bitcast(X4), scales=q_scales[:], in_=q_grp[:].rearrange("p c q t -> p (c q t)")
+        )
+        k_words = sbt([P, I], U32, "k_words")
+        nc.vector.tensor_copy(k_words[:], word_win[:].bitcast(U32).indirect(offsets[:]))
+
+        mark_cols = []
+        for name, win, bank_tag in (("x", x_win, "bank_w"), ("y", y_win, "bank_o3")):
+            picked = sbt([P, I], F32, name + "_picked")
+            nc.scalar.activation(picked[:], win[:].indirect(offsets[:]), ACT.Copy)
+            bank = ps.tile([P, 4, P], F32, name=name + "_bank", tag=bank_tag)
+            for j in range(4):
+                nc.tensor.transpose(bank[:, j, :], picked[:, j * P : (j + 1) * P], ident[:])
+            cols = sbt([P, 4, 1], F32, name + "_cols")
+            nc.scalar.copy(cols[:], bank[:, :, 0:1])
+            mark_cols.append(cols)
+        x_cols, y_cols = mark_cols
+
+        v_win = [sbt([P, T], F32, "v_win%d" % b, "slot%d" % b) for b in range(4)]
+        for b in range(4):
+            nc.sync.dma_start(out=v_win[b][:], in_=vals[b * P : (b + 1) * P, :])
+
+        ab = []
+        for c, name in enumerate(("a", "b")):
+            bank = ps.tile([P, 4, Q], F32, name=name + "_bank")
+            for j in range(4):
+                nc.tensor.matmul_mx(
+                    out=bank[:, j, :],
+                    lhsT=k_words[:, j * P : (j + 1) * P].bitcast(X4),
+                    lhsT_scale=k_scales[:, j * P : (j + 1) * P],
+                    rhs=q_codes[:, c * Q : (c + 1) * Q].bitcast(X4),
+                    rhs_scale=q_scales[:, c * Q : (c + 1) * Q],
+                    start=True,
+                    stop=True,
+                )
+            ab.append(bank)
+        dx2 = sbt([P, 4, Q], F32, "dx2")
+        for j in range(4):
+            nc.scalar.activation(dx2[:, j, :], ab[0][:, j, :], ACT.Square, bias=x_cols[:, j, :], scale=-1.0)
+        dy = sbt([P, 4, Q], F32, "dy", "dy_before")
+        dy2 = sbt([P, 4, Q], F32, "dy2")
+        nc.vector.tensor_tensor(dy[:], ab[1][:], y_cols[:].broadcast_to([P, 4, Q]), ALU.subtract)
+        nc.vector.tensor_tensor(dy2[:], dy[:], dy[:], ALU.mult)
+
+        before_sb = sbt([P, E], F32, "before_sb", "dy_before")
+        nc.sync.dma_start(out=before_sb[:], in_=before)
+
+        dist = ps.tile([P, 4, P], F32, name="dist")
+        for c, part in enumerate((dx2, dy2)):
+            for j in range(4):
+                nc.tensor.matmul(
+                    dist[:, j, :], part[:, j, :], ident[:], is_transpose=True,
+                    start=(c == 0 and j == 0), stop=(c == 1 and j == 3),
+                )
+
+        def gather_values(b, engines):
+            picked = sbt([P, I], BF16, "v_picked%d" % b)
+            n = I // len(engines)
+            for h, eng in enumerate(engines):
+                src = v_win[b][:].indirect(offsets[:, h * n // 16 : (h + 1) * n // 16])
+                if eng == "vector":
+                    nc.vector.tensor_copy(picked[:, h * n : (h + 1) * n], src)
+                else:
+                    nc.scalar.activation(picked[:, h * n : (h + 1) * n], src, ACT.Copy)
+            return picked
+
+        def turn_values(b, picked):
+            words = picked[:].bitcast(F32)
+            bank = ps.tile([P, 2, P], F32, name="v_bank%d" % b, tag="v_bank%d" % (b % 2))
+            for u in range(2):
+                nc.tensor.transpose(bank[:, u, :], words[:, u : I // 2 : 2], ident[:])
+            grp = sbt([P, P, PACK], BF16, "v_grp%d" % b)
+            nc.scalar.copy(grp[:].bitcast(F32), bank[:].rearrange("p u e -> p e u"))
+            return grp
+
+        def quantise_values(b, grp):
+            codes = sbt([P, P], U32, "v_codes%d" % b)
+            scales = sbt([P, P], U8, "v_scales%d" % b)
+            nc.vector.quantize_mx(out=codes[:].bitcast(X4), scales=scales[:], in_=grp[:].rearrange("p e t -> p (e t)"))
+            return codes, scales
+
+        picked0 = gather_values(0, ["vector"])
+
+        p_t = sbt([P, PACK, P], F32, "p_t")
+        z0 = sbt([P, 1], F32, "z0")
+        nc.scalar.activation(
+            p_t[:], dist[:].rearrange("q j m -> q (j m)").rearrange("q (s t) -> q t s", t=PACK), ACT.Exp, scale=neg_lam[:], accum_out=z0[:]
+        )
+        pg = sbt([P, G], F32, "pg")
+        nc.vector.tensor_reduce(pg[:], p_t[:].rearrange("q t (g h) -> q g t h", h=2), AX.XY, ALU.add)
+        rest = sbt([P, G], F32, "rest")
+        nc.vector.tensor_scalar(rest[:], pg[:], -1.0, z0[:], ALU.mult, ALU.add)
+        k0 = sbt([P, G], F32, "k0")
+        nc.vector.reciprocal(k0[:], rest[:])
+        w = sbt([P, PACK, P], F32, "w")
+        nc.vector.tensor_tensor(
+            w[:].rearrange("q t (g h) -> q t g h", h=2),
+            p_t[:].rearrange("q t (g h) -> q t g h", h=2),
+            k0[:].unsqueeze(1).unsqueeze(3).broadcast_to([P, PACK, G, 2]),
+            ALU.mult,
+        )
+        grp0 = turn_values(0, picked0)
+        picked1 = gather_values(1, ["scalar"])
+        w_bank = ps.tile([P, PACK, Q], F32, name="w_bank", tag="bank_w")
+        for t in range(PACK):
+            nc.tensor.transpose(w_bank[:, t, :], w[:, t, :], ident[:])
+        v_q = [quantise_values(0, grp0)]
+        grp1 = turn_values(1, picked1)
+        picked2 = gather_values(2, ["scalar"])
+        w_grp = sbt([P, Q, PACK], BF16, "w_grp")
+        nc.vector.tensor_tensor(
+            w_grp[:], w_bank[:].rearrange("p t q -> p q t"),
+            os_col[:].unsqueeze(1).broadcast_to([P, Q, PACK]), ALU.mult,
+        )
+        v_q.append(quantise_values(1, grp1))
+        w_codes = sbt([P, Q], U32, "w_codes")
+        w_scales = sbt([P, Q], U8, "w_scales")
+        nc.vector.quantize_mx(out=w_codes[:].bitcast(X4), scales=w_scales[:], in_=w_grp[:].rearrange("p q t -> p (q t)"))
+        grp2 = turn_values(2, picked2)
+        v_q.append(quantise_values(2, grp2))
+
+        def product(dst, b):
+            nc.tensor.matmul_mx(
+                out=dst, lhsT=w_codes[:].bitcast(X4), lhsT_scale=w_scales[:],
+                rhs=v_q[b][0][:].bitcast(X4), rhs_scale=v_q[b][1][:], start=True, stop=True,
+            )
+
+        o_head = ps.tile([P, 3, P], F32, name="o_head")
+        for b in range(3):
+            product(o_head[:, b, :], b)
+        new_head = sbt([P, 3 * P], F32, "new_head")
+        nc.scalar.activation(new_head[:], o_head[:].rearrange("q b e -> q (b e)"), ACT.Copy, scale=keep_new[:])
+
+        picked3 = gather_values(3, ["vector", "scalar"])
+        old_tail = sbt([P, P], F32, "old_tail")
+        nc.scalar.activation(old_tail[:], before_sb[:, 3 * P :], ACT.Copy, scale=hold_col[:])
+        y_head = sbt([P, 3 * P], F32, "y_head")
+        nc.vector.scalar_tensor_tensor(y_head[:], before_sb[:, : 3 * P], hold_col[:], new_head[:], ALU.mult, ALU.add)
+        nc.sync.dma_start(out=out[:, : 3 * P], in_=y_head[:])
+
+        grp3 = turn_values(3, picked3)
+        v_q.append(quantise_values(3, grp3))
+        o_tail = ps.tile([P, P], F32, name="o_tail", tag="bank_o3")
+        product(o_tail[:], 3)
+        y_tail = sbt([P, P], F32, "y_tail")
+        nc.vector.scalar_tensor_tensor(y_tail[:], o_tail[:], keep_new[:], old_tail[:], ALU.mult, ALU.add)
+        nc.sync.dma_start(out=out[:, 3 * P :], in_=y_tail[:])

@@ -6,6 +6,7 @@ from concourse.masks import make_identity
 D, T, I, Q, E, G = 512, 2048, 512, 128, 512, 64
 P = 128
 PACK = 4
+HALF = I // 2
 FLOPS = 2 * D * Q * I * 2 + 2 * I * Q * E
 
 F32 = mybir.dt.float32
@@ -32,50 +33,67 @@ def tile_attend_maplace_outside_blend_kernel(
         def sbt(shape, dtype, name, tag=None):
             return sb.tile(shape, dtype, name=name, tag=tag or name, align_bytes=64)
 
+        def bank(shape, name, number):
+            return ps.tile(shape, F32, name=name, tag="bank%d" % number)
+
         offsets = lists.tile([P, I // 16], U16, name="offsets")
         nc.sync.dma_start(offsets[:], offs)
 
-        scale_win = sbt([P, T], U8, "scale_win", "slot0")
-        x_win = sbt([P, T], F32, "x_win", "slot1")
-        y_win = sbt([P, T], F32, "y_win", "slot2")
-        word_win = sbt([P, T], I32, "word_win", "slot3")
-        nc.vector.memset(scale_win[:].bitcast(I32), 0)
-        nc.vector.memset(x_win[:], 0.0)
-        nc.vector.memset(y_win[:], 0.0)
+        def listed(window, first, count):
+            return window.indirect(offsets[:, first // 16 : (first + count) // 16])
+
+        scale_win = sbt([P, T], U8, "scale_win")
+        x_win = sbt([P, T + 1], F32, "x_win")
+        y_win = sbt([P, T + 1], F32, "y_win")
+        word_win = sbt([P, T], I32, "word_win", "words_then")
+        nc.gpsimd.memset(scale_win[:].bitcast(I32), 0)
+        for win, split in ((y_win, 1024), (x_win, 768)):
+            nc.gpsimd.memset(win[:, :split], 0.0)
+            nc.vector.memset(win[:, split:], 0.0)
 
         q_raw = [sbt([P, PACK, Q], F32, "q_raw%d" % c) for c in range(2)]
-        for raw, src in zip(q_raw, (query, query2)):
-            nc.scalar.dma_start(out=raw[:], in_=src.rearrange("(p t) q -> p t q", t=PACK))
-        nc.scalar.dma_start(out=word_win[:], in_=keys_words[0].rearrange("p n t -> p (n t)").bitcast(I32))
-
+        nc.sync.dma_start(out=q_raw[0][:], in_=query.rearrange("(p t) q -> p t q", t=PACK))
         scale_rows = keys_scales[0].bitcast(I32).rearrange("(quad r) c -> r quad c", r=4)
         for r in range(4):
             nc.sync.dma_start(out=scale_win[r:P:32, :].bitcast(I32), in_=scale_rows[r])
-        nc.sync.dma_start(out=x_win[0:1, :], in_=xmark[0:1, :])
-        nc.sync.dma_start(out=y_win[0:1, :], in_=ymark[0:1, :])
-
-        ident = sbt([P, P], F32, "ident")
-        make_identity(nc, ident[:])
+        key_words = keys_words[0].rearrange("p n t -> p (n t)").bitcast(I32)
+        nc.sync.dma_start(out=word_win[:, : T // 2], in_=key_words[:, : T // 2])
+        nc.sync.dma_start(out=y_win[0:1, :T], in_=ymark[0:1, :])
+        nc.sync.dma_start(out=x_win[0:1, :T], in_=xmark[0:1, :])
+        nc.sync.dma_start(out=q_raw[1][:], in_=query2.rearrange("(p t) q -> p t q", t=PACK))
+        nc.sync.dma_start(out=word_win[:, T // 2 :], in_=key_words[:, T // 2 :])
+        v_win = [sbt([P, T], F32, "v_win%d" % b, "v_win%d_then" % b) for b in range(4)]
         lam_col = sbt([P, 1], F32, "lam_col")
         hold_col = sbt([P, 1], F32, "hold_col")
         os_col = sbt([P, PACK], F32, "os_col")
-        nc.gpsimd.dma_start(out=lam_col[:], in_=lam)
-        nc.gpsimd.dma_start(out=hold_col[:], in_=hold)
-        nc.gpsimd.dma_start(out=os_col[:], in_=slot_factor.rearrange("o (p t) -> p (o t)", t=PACK))
-        neg_lam = sbt([P, 1], F32, "neg_lam")
+        before_sb = sbt([P, E], F32, "before_sb")
+        riders = (
+            (lam_col, lam),
+            (os_col, slot_factor.rearrange("o (p t) -> p (o t)", t=PACK)),
+            (hold_col, hold),
+            (before_sb, before),
+        )
+        for b, (dst, src) in enumerate(riders):
+            nc.sync.dma_start(out=v_win[b][:], in_=vals[b * P : (b + 1) * P, :])
+            nc.sync.dma_start(out=dst[:], in_=src)
+
+        ident = sbt([P, P], F32, "ident")
+        make_identity(nc, ident[:])
+        neg_lam = sbt([P, 1], F32, "neg_lam", "lam_then_values")
         keep_new = sbt([P, 1], F32, "keep_new")
         nc.gpsimd.tensor_scalar(neg_lam[:], lam_col[:], -1.0, 0.0, ALU.mult, ALU.add)
         nc.gpsimd.tensor_scalar(keep_new[:], hold_col[:], -1.0, 1.0, ALU.mult, ALU.add)
 
         q_grp = sbt([P, 2, Q, PACK], BF16, "q_grp")
+        nc.scalar.activation(q_grp[:, 0], q_raw[0][:].rearrange("p t q -> p q t"), ACT.Copy)
         q_codes = sbt([P, 2 * Q], U32, "q_codes")
         q_scales = sbt([P, 2 * Q], U8, "q_scales")
-        nc.vector.tensor_copy(
-            out=q_grp[:, 0].rearrange("p (c i) t -> p c t i", i=4),
-            in_=q_raw[0][:].rearrange("p t (c i) -> p c t i", i=4),
-        )
         k_scales = sbt([P, I], U8, "k_scales")
-        nc.vector.tensor_copy(k_scales[:], scale_win[:].indirect(offsets[:]))
+        nc.vector.tensor_copy(k_scales[:], listed(scale_win[:], 0, I))
+        y_picked = sbt([P, I], F32, "y_picked")
+        x_picked = sbt([P, I], F32, "x_picked")
+        nc.scalar.activation(y_picked[:], listed(y_win[:], 0, I), ACT.Copy)
+        nc.vector.tensor_copy(x_picked[:], listed(x_win[:], 0, I))
         nc.vector.tensor_copy(
             out=q_grp[:, 1].rearrange("p (c i) t -> p c t i", i=4),
             in_=q_raw[1][:].rearrange("p t (c i) -> p c t i", i=4),
@@ -83,147 +101,143 @@ def tile_attend_maplace_outside_blend_kernel(
         nc.vector.quantize_mx(
             out=q_codes[:].bitcast(X4), scales=q_scales[:], in_=q_grp[:].rearrange("p c q t -> p (c q t)")
         )
+
+        marks = []
+        for c, picked in ((1, y_picked), (0, x_picked)):
+            turned = bank([P, 4, P], "mark_bank%d" % c, c)
+            for j in range(4):
+                nc.tensor.transpose(turned[:, j, :], picked[:, j * P : (j + 1) * P], ident[:])
+            cols = sbt([P, 4, 1], F32, "mark_cols%d" % c)
+            nc.scalar.copy(cols[:], turned[:, :, 0:1])
+            marks.insert(0, cols)
+
         k_words = sbt([P, I], U32, "k_words")
-        nc.vector.tensor_copy(k_words[:], word_win[:].bitcast(U32).indirect(offsets[:]))
+        for h in range(2):
+            nc.vector.tensor_copy(k_words[:, h * HALF : (h + 1) * HALF], listed(word_win[:].bitcast(U32), h * HALF, HALF))
 
-        mark_cols = []
-        for name, win, bank_tag in (("x", x_win, "bank_w"), ("y", y_win, "bank_o3")):
-            picked = sbt([P, I], F32, name + "_picked")
-            nc.scalar.activation(picked[:], win[:].indirect(offsets[:]), ACT.Copy)
-            bank = ps.tile([P, 4, P], F32, name=name + "_bank", tag=bank_tag)
-            for j in range(4):
-                nc.tensor.transpose(bank[:, j, :], picked[:, j * P : (j + 1) * P], ident[:])
-            cols = sbt([P, 4, 1], F32, name + "_cols")
-            nc.scalar.copy(cols[:], bank[:, :, 0:1])
-            mark_cols.append(cols)
-        x_cols, y_cols = mark_cols
-
-        v_win = [sbt([P, T], F32, "v_win%d" % b, "slot%d" % b) for b in range(4)]
-        for b in range(4):
-            nc.sync.dma_start(out=v_win[b][:], in_=vals[b * P : (b + 1) * P, :])
-
-        ab = []
-        for c, name in enumerate(("a", "b")):
-            bank = ps.tile([P, 4, Q], F32, name=name + "_bank")
-            for j in range(4):
-                nc.tensor.matmul_mx(
-                    out=bank[:, j, :],
-                    lhsT=k_words[:, j * P : (j + 1) * P].bitcast(X4),
-                    lhsT_scale=k_scales[:, j * P : (j + 1) * P],
-                    rhs=q_codes[:, c * Q : (c + 1) * Q].bitcast(X4),
-                    rhs_scale=q_scales[:, c * Q : (c + 1) * Q],
-                    start=True,
-                    stop=True,
-                )
-            ab.append(bank)
-        dx2 = sbt([P, 4, Q], F32, "dx2")
+        squares = []
         for j in range(4):
-            nc.scalar.activation(dx2[:, j, :], ab[0][:, j, :], ACT.Square, bias=x_cols[:, j, :], scale=-1.0)
-        dy = sbt([P, 4, Q], F32, "dy", "dy_before")
-        dy2 = sbt([P, 4, Q], F32, "dy2")
-        nc.vector.tensor_tensor(dy[:], ab[1][:], y_cols[:].broadcast_to([P, 4, Q]), ALU.subtract)
-        nc.vector.tensor_tensor(dy2[:], dy[:], dy[:], ALU.mult)
+            point = bank([P, 2, Q], "point%d" % j, 2 + j)
+            nc.tensor.matmul_mx(
+                out=point[:].rearrange("s c q -> s (c q)"),
+                lhsT=k_words[:, j * P : (j + 1) * P].bitcast(X4),
+                lhsT_scale=k_scales[:, j * P : (j + 1) * P],
+                rhs=q_codes[:].bitcast(X4),
+                rhs_scale=q_scales[:],
+                start=True,
+                stop=True,
+            )
+            square = sbt([P, 2, Q], F32, "square%d" % j)
+            for c in range(2):
+                nc.scalar.activation(square[:, c, :], point[:, c, :], ACT.Square, bias=marks[c][:, j, :], scale=-1.0)
+            squares.append(square)
 
-        before_sb = sbt([P, E], F32, "before_sb", "dy_before")
-        nc.sync.dma_start(out=before_sb[:], in_=before)
+        def gather_values(b, picked, engine, first, count):
+            src = listed(v_win[b][:], first, count)
+            if engine == "vector":
+                nc.vector.tensor_copy(picked[:, first : first + count], src)
+            else:
+                nc.scalar.activation(picked[:, first : first + count], src, ACT.Copy)
 
-        dist = ps.tile([P, 4, P], F32, name="dist")
-        for c, part in enumerate((dx2, dy2)):
-            for j in range(4):
-                nc.tensor.matmul(
-                    dist[:, j, :], part[:, j, :], ident[:], is_transpose=True,
-                    start=(c == 0 and j == 0), stop=(c == 1 and j == 3),
-                )
-
-        def gather_values(b, engines):
-            picked = sbt([P, I], BF16, "v_picked%d" % b)
-            n = I // len(engines)
-            for h, eng in enumerate(engines):
-                src = v_win[b][:].indirect(offsets[:, h * n // 16 : (h + 1) * n // 16])
-                if eng == "vector":
-                    nc.vector.tensor_copy(picked[:, h * n : (h + 1) * n], src)
-                else:
-                    nc.scalar.activation(picked[:, h * n : (h + 1) * n], src, ACT.Copy)
-            return picked
-
-        def turn_values(b, picked):
-            words = picked[:].bitcast(F32)
-            bank = ps.tile([P, 2, P], F32, name="v_bank%d" % b, tag="v_bank%d" % (b % 2))
-            for u in range(2):
-                nc.tensor.transpose(bank[:, u, :], words[:, u : I // 2 : 2], ident[:])
-            grp = sbt([P, P, PACK], BF16, "v_grp%d" % b)
-            nc.scalar.copy(grp[:].bitcast(F32), bank[:].rearrange("p u e -> p e u"))
-            return grp
-
-        def quantise_values(b, grp):
-            codes = sbt([P, P], U32, "v_codes%d" % b)
-            scales = sbt([P, P], U8, "v_scales%d" % b)
-            nc.vector.quantize_mx(out=codes[:].bitcast(X4), scales=scales[:], in_=grp[:].rearrange("p e t -> p (e t)"))
-            return codes, scales
-
-        picked0 = gather_values(0, ["vector"])
+        picked0 = sbt([P, I], BF16, "v_picked0", "words_then")
+        gather_values(0, picked0, "vector", 0, I)
 
         p_t = sbt([P, PACK, P], F32, "p_t")
-        z0 = sbt([P, 1], F32, "z0")
-        nc.scalar.activation(
-            p_t[:], dist[:].rearrange("q j m -> q (j m)").rearrange("q (s t) -> q t s", t=PACK), ACT.Exp, scale=neg_lam[:], accum_out=z0[:]
-        )
-        pg = sbt([P, G], F32, "pg")
-        nc.vector.tensor_reduce(pg[:], p_t[:].rearrange("q t (g h) -> q g t h", h=2), AX.XY, ALU.add)
-        rest = sbt([P, G], F32, "rest")
-        nc.vector.tensor_scalar(rest[:], pg[:], -1.0, z0[:], ALU.mult, ALU.add)
-        k0 = sbt([P, G], F32, "k0")
-        nc.vector.reciprocal(k0[:], rest[:])
-        w = sbt([P, PACK, P], F32, "w")
-        nc.vector.tensor_tensor(
-            w[:].rearrange("q t (g h) -> q t g h", h=2),
-            p_t[:].rearrange("q t (g h) -> q t g h", h=2),
-            k0[:].unsqueeze(1).unsqueeze(3).broadcast_to([P, PACK, G, 2]),
-            ALU.mult,
-        )
-        grp0 = turn_values(0, picked0)
-        picked1 = gather_values(1, ["scalar"])
-        w_bank = ps.tile([P, PACK, Q], F32, name="w_bank", tag="bank_w")
+        z = [sbt([P, 1], F32, "z%d" % h, "z%d_then" % h) for h in range(2)]
+        neg_pg = sbt([P, G], F32, "neg_pg", "v_win0_then")
+        for h in range(2):
+            dist = bank([P, 2, P], "dist%d" % h, 6 + h)
+            for j in range(2):
+                for c in range(2):
+                    nc.tensor.matmul(
+                        dist[:, j, :], squares[2 * h + j][:, c, :], ident[:], is_transpose=True,
+                        start=(c == 0), stop=(c == 1),
+                    )
+            p_half = p_t[:, :, h * P // 2 : (h + 1) * P // 2]
+            nc.scalar.activation(
+                p_half, dist[:].rearrange("q j m -> q (j m)").rearrange("q (s t) -> q t s", t=PACK),
+                ACT.Exp, scale=neg_lam[:], accum_out=z[h][:],
+            )
+            nc.vector.tensor_reduce(
+                neg_pg[:, h * G // 2 : (h + 1) * G // 2], p_half.rearrange("q t (g r) -> q g t r", r=2), AX.XY, ALU.add,
+                negate=True,
+            )
+
+        def turn_values(b, picked, grp):
+            words = picked[:].bitcast(F32)
+            turned = bank([P, 2, P], "v_bank%d" % b, (7, 6, 4, 2)[b])
+            for u in range(2):
+                nc.tensor.transpose(turned[:, u, :], words[:, u : I // 2 : 2], ident[:])
+            nc.scalar.copy(grp.bitcast(F32), turned[:].rearrange("p u e -> p e u"))
+
+        def quantise_values(b, grp, codes):
+            scales = sbt([P, P], U8, "v_scales%d" % b)
+            nc.vector.quantize_mx(out=codes.bitcast(X4), scales=scales[:], in_=grp.rearrange("p e t -> p (e t)"))
+            return codes, scales
+
+        p_bank = bank([P, PACK, Q], "p_bank", 4)
         for t in range(PACK):
-            nc.tensor.transpose(w_bank[:, t, :], w[:, t, :], ident[:])
-        v_q = [quantise_values(0, grp0)]
-        grp1 = turn_values(1, picked1)
-        picked2 = gather_values(2, ["scalar"])
-        w_grp = sbt([P, Q, PACK], BF16, "w_grp")
+            nc.tensor.transpose(p_bank[:, t, :], p_t[:, t, :], ident[:])
+
+        grp0 = sbt([P, P, PACK], BF16, "v_grp0")
+        turn_values(0, picked0, grp0[:])
+        picked1 = sbt([P, I], BF16, "v_picked1", "lam_then_values")
+        gather_values(1, picked1, "scalar", 0, I)
+
+        rest = sbt([P, G], F32, "rest")
+        nc.vector.tensor_scalar(rest[:], neg_pg[:], z[0][:], z[1][:], ALU.add, ALU.add)
+        k0 = sbt([P, G, 1], F32, "k0", "k0_then")
+        nc.vector.reciprocal(k0[:, :, 0], rest[:])
+        k2 = sbt([P, G, 2], F32, "k2")
+        nc.vector.tensor_copy(k2[:], k0[:].broadcast_to([P, G, 2]))
+        k_bank = bank([P, Q], "k_bank", 5)
+        nc.tensor.transpose(k_bank[:], k2[:].rearrange("q g r -> q (g r)"), ident[:])
+        po = sbt([P, Q, PACK], F32, "po")
         nc.vector.tensor_tensor(
-            w_grp[:], w_bank[:].rearrange("p t q -> p q t"),
-            os_col[:].unsqueeze(1).broadcast_to([P, Q, PACK]), ALU.mult,
+            po[:], p_bank[:].rearrange("s t q -> s q t"), os_col[:].unsqueeze(1).broadcast_to([P, Q, PACK]), ALU.mult
         )
-        v_q.append(quantise_values(1, grp1))
+        picked2 = sbt([P, I], BF16, "v_picked2", "z1_then")
+        gather_values(2, picked2, "scalar", 0, I)
+        grp1 = sbt([P, P, PACK], BF16, "v_grp1", "v_win2_then")
+        turn_values(1, picked1, grp1[:])
+        picked3 = sbt([P, I], BF16, "v_picked3", "k0_then")
+        gather_values(3, picked3, "vector", 0, HALF)
+        gather_values(3, picked3, "scalar", HALF, HALF)
+        late = sbt([P, 2, P, PACK], BF16, "late", "v_win3_then")
+        w_grp, grp2 = late[:, 0], late[:, 1]
+        nc.vector.tensor_tensor(w_grp, k_bank[:].unsqueeze(2).broadcast_to([P, Q, PACK]), po[:], ALU.mult)
         w_codes = sbt([P, Q], U32, "w_codes")
         w_scales = sbt([P, Q], U8, "w_scales")
-        nc.vector.quantize_mx(out=w_codes[:].bitcast(X4), scales=w_scales[:], in_=w_grp[:].rearrange("p q t -> p (q t)"))
-        grp2 = turn_values(2, picked2)
-        v_q.append(quantise_values(2, grp2))
+        nc.vector.quantize_mx(out=w_codes[:].bitcast(X4), scales=w_scales[:], in_=w_grp.rearrange("p q t -> p (q t)"))
+        head_codes = sbt([P, 3, P], U32, "head_codes")
+        v_q = [quantise_values(0, grp0[:], head_codes[:, 0, :]), quantise_values(1, grp1[:], head_codes[:, 1, :])]
+        turn_values(2, picked2, grp2)
+        grp3 = sbt([P, P, PACK], BF16, "v_grp3")
+        turn_values(3, picked3, grp3[:])
+        v_q.append(quantise_values(2, grp2, head_codes[:, 2, :]))
 
         def product(dst, b):
             nc.tensor.matmul_mx(
                 out=dst, lhsT=w_codes[:].bitcast(X4), lhsT_scale=w_scales[:],
-                rhs=v_q[b][0][:].bitcast(X4), rhs_scale=v_q[b][1][:], start=True, stop=True,
+                rhs=v_q[b][0].bitcast(X4), rhs_scale=v_q[b][1][:], start=True, stop=True,
             )
 
-        o_head = ps.tile([P, 3, P], F32, name="o_head")
+        o_head = bank([P, 3, P], "o_head", 4)
         for b in range(3):
             product(o_head[:, b, :], b)
-        new_head = sbt([P, 3 * P], F32, "new_head")
-        nc.scalar.activation(new_head[:], o_head[:].rearrange("q b e -> q (b e)"), ACT.Copy, scale=keep_new[:])
 
-        picked3 = gather_values(3, ["vector", "scalar"])
-        old_tail = sbt([P, P], F32, "old_tail")
-        nc.scalar.activation(old_tail[:], before_sb[:, 3 * P :], ACT.Copy, scale=hold_col[:])
+        kept = sbt([P, E], F32, "kept")
+        nc.gpsimd.tensor_scalar(kept[:], before_sb[:], hold_col[:], 0.0, ALU.mult, ALU.add)
         y_head = sbt([P, 3 * P], F32, "y_head")
-        nc.vector.scalar_tensor_tensor(y_head[:], before_sb[:, : 3 * P], hold_col[:], new_head[:], ALU.mult, ALU.add)
+        nc.vector.scalar_tensor_tensor(
+            y_head[:], o_head[:].rearrange("q b e -> q (b e)"), keep_new[:], kept[:, : 3 * P], ALU.mult, ALU.add
+        )
         nc.sync.dma_start(out=out[:, : 3 * P], in_=y_head[:])
 
-        grp3 = turn_values(3, picked3)
-        v_q.append(quantise_values(3, grp3))
-        o_tail = ps.tile([P, P], F32, name="o_tail", tag="bank_o3")
+        tail_codes = sbt([P, P], U32, "tail_codes")
+        v_q.append(quantise_values(3, grp3[:], tail_codes[:]))
+        o_tail = bank([P, P], "o_tail", 1)
         product(o_tail[:], 3)
         y_tail = sbt([P, P], F32, "y_tail")
-        nc.vector.scalar_tensor_tensor(y_tail[:], o_tail[:], keep_new[:], old_tail[:], ALU.mult, ALU.add)
+        nc.vector.scalar_tensor_tensor(y_tail[:], o_tail[:], keep_new[:], kept[:, 3 * P :], ALU.mult, ALU.add)
         nc.sync.dma_start(out=out[:, 3 * P :], in_=y_tail[:])

@@ -43,7 +43,7 @@ def tile_attend_maplace_outside_blend_kernel(
             return window.indirect(offsets[:, first // 16 : (first + count) // 16])
 
         scale_win = sbt([P, T], U8, "scale_win")
-        x_win = sbt([P, T + 1], F32, "x_win")
+        x_win = sbt([P, T + 1], F32, "x_win", "x_win_then")
         y_win = sbt([P, T + 1], F32, "y_win")
         word_win = sbt([P, T], I32, "word_win", "words_then")
         nc.gpsimd.memset(scale_win[:].bitcast(I32), 0)
@@ -59,8 +59,8 @@ def tile_attend_maplace_outside_blend_kernel(
         key_words = keys_words[0].rearrange("p n t -> p (n t)").bitcast(I32)
         nc.sync.dma_start(out=word_win[:, : T // 2], in_=key_words[:, : T // 2])
         nc.sync.dma_start(out=y_win[0:1, :T], in_=ymark[0:1, :])
-        nc.sync.dma_start(out=x_win[0:1, :T], in_=xmark[0:1, :])
         nc.sync.dma_start(out=q_raw[1][:], in_=query2.rearrange("(p t) q -> p t q", t=PACK))
+        nc.sync.dma_start(out=x_win[0:1, :T], in_=xmark[0:1, :])
         nc.sync.dma_start(out=word_win[:, T // 2 :], in_=key_words[:, T // 2 :])
         v_win = [sbt([P, T], F32, "v_win%d" % b, "v_win%d_then" % b) for b in range(4)]
         lam_col = sbt([P, 1], F32, "lam_col")
@@ -92,8 +92,8 @@ def tile_attend_maplace_outside_blend_kernel(
         nc.vector.tensor_copy(k_scales[:], listed(scale_win[:], 0, I))
         y_picked = sbt([P, I], F32, "y_picked")
         x_picked = sbt([P, I], F32, "x_picked")
-        nc.scalar.activation(y_picked[:], listed(y_win[:], 0, I), ACT.Copy)
-        nc.vector.tensor_copy(x_picked[:], listed(x_win[:], 0, I))
+        nc.vector.tensor_copy(y_picked[:], listed(y_win[:], 0, I))
+        nc.scalar.activation(x_picked[:], listed(x_win[:], 0, I), ACT.Copy)
         nc.vector.tensor_copy(
             out=q_grp[:, 1].rearrange("p (c i) t -> p c t i", i=4),
             in_=q_raw[1][:].rearrange("p t (c i) -> p c t i", i=4),
@@ -107,7 +107,7 @@ def tile_attend_maplace_outside_blend_kernel(
             turned = bank([P, 4, P], "mark_bank%d" % c, c)
             for j in range(4):
                 nc.tensor.transpose(turned[:, j, :], picked[:, j * P : (j + 1) * P], ident[:])
-            cols = sbt([P, 4, 1], F32, "mark_cols%d" % c)
+            cols = sbt([P, 4, 1], F32, "mark_cols%d" % c, "x_win_then" if c == 1 else None)
             nc.scalar.copy(cols[:], turned[:, :, 0:1])
             marks.insert(0, cols)
 
@@ -200,21 +200,21 @@ def tile_attend_maplace_outside_blend_kernel(
         gather_values(2, picked2, "scalar", 0, I)
         grp1 = sbt([P, P, PACK], BF16, "v_grp1", "v_win2_then")
         turn_values(1, picked1, grp1[:])
+        w_grp = sbt([P, Q, PACK], BF16, "w_grp")
+        nc.vector.tensor_tensor(w_grp[:], k_bank[:].unsqueeze(2).broadcast_to([P, Q, PACK]), po[:], ALU.mult)
+        w_codes = sbt([P, Q], U32, "w_codes")
+        w_scales = sbt([P, Q], U8, "w_scales")
+        nc.vector.quantize_mx(out=w_codes[:].bitcast(X4), scales=w_scales[:], in_=w_grp[:].rearrange("p q t -> p (q t)"))
+        head_codes = sbt([P, 3, P], U32, "head_codes")
+        v_q = [quantise_values(0, grp0[:], head_codes[:, 0, :]), quantise_values(1, grp1[:], head_codes[:, 1, :])]
         picked3 = sbt([P, I], BF16, "v_picked3", "k0_then")
         gather_values(3, picked3, "vector", 0, HALF)
         gather_values(3, picked3, "scalar", HALF, HALF)
-        late = sbt([P, 2, P, PACK], BF16, "late", "v_win3_then")
-        w_grp, grp2 = late[:, 0], late[:, 1]
-        nc.vector.tensor_tensor(w_grp, k_bank[:].unsqueeze(2).broadcast_to([P, Q, PACK]), po[:], ALU.mult)
-        w_codes = sbt([P, Q], U32, "w_codes")
-        w_scales = sbt([P, Q], U8, "w_scales")
-        nc.vector.quantize_mx(out=w_codes[:].bitcast(X4), scales=w_scales[:], in_=w_grp.rearrange("p q t -> p (q t)"))
-        head_codes = sbt([P, 3, P], U32, "head_codes")
-        v_q = [quantise_values(0, grp0[:], head_codes[:, 0, :]), quantise_values(1, grp1[:], head_codes[:, 1, :])]
-        turn_values(2, picked2, grp2)
+        grp2 = sbt([P, P, PACK], BF16, "v_grp2", "v_win3_then")
+        turn_values(2, picked2, grp2[:])
         grp3 = sbt([P, P, PACK], BF16, "v_grp3")
         turn_values(3, picked3, grp3[:])
-        v_q.append(quantise_values(2, grp2, head_codes[:, 2, :]))
+        v_q.append(quantise_values(2, grp2[:], head_codes[:, 2, :]))
 
         def product(dst, b):
             nc.tensor.matmul_mx(

@@ -28,6 +28,7 @@ def tile_attend_maplace_outside_blend_kernel(
     with ExitStack() as ctx:
         lists = ctx.enter_context(tc.tile_pool(name="lists", bufs=1))
         sb = ctx.enter_context(tc.tile_pool(name="sb", bufs=1))
+        last = ctx.enter_context(tc.tile_pool(name="last", bufs=1))
         ps = ctx.enter_context(tc.psum_pool(name="ps", bufs=1))
 
         def sbt(shape, dtype, name, tag=None):
@@ -62,20 +63,22 @@ def tile_attend_maplace_outside_blend_kernel(
         nc.sync.dma_start(out=q_raw[1][:], in_=query2.rearrange("(p t) q -> p t q", t=PACK))
         nc.sync.dma_start(out=x_win[0:1, :T], in_=xmark[0:1, :])
         nc.sync.dma_start(out=word_win[:, T // 2 :], in_=key_words[:, T // 2 :])
-        v_win = [sbt([P, T], F32, "v_win%d" % b, "v_win%d_then" % b) for b in range(4)]
+        v_win = [sbt([P, T], F32, "v_win%d" % b, "v_win%d_then" % b) for b in range(3)]
+        v_win.append(last.tile([P, T], F32, name="v_win3", align_bytes=64, offset=0))
         lam_col = sbt([P, 1], F32, "lam_col")
         hold_col = sbt([P, 1], F32, "hold_col")
         os_col = sbt([P, PACK], F32, "os_col")
         before_sb = sbt([P, E], F32, "before_sb")
         riders = (
-            (lam_col, lam),
-            (os_col, slot_factor.rearrange("o (p t) -> p (o t)", t=PACK)),
-            (hold_col, hold),
-            (before_sb, before),
+            [(lam_col, lam)],
+            [(os_col, slot_factor.rearrange("o (p t) -> p (o t)", t=PACK))],
+            [],
+            [(hold_col, hold), (before_sb, before)],
         )
-        for b, (dst, src) in enumerate(riders):
+        for b, followers in enumerate(riders):
             nc.sync.dma_start(out=v_win[b][:], in_=vals[b * P : (b + 1) * P, :])
-            nc.sync.dma_start(out=dst[:], in_=src)
+            for dst, src in followers:
+                nc.sync.dma_start(out=dst[:], in_=src)
 
         ident = sbt([P, P], F32, "ident")
         make_identity(nc, ident[:])
@@ -205,12 +208,12 @@ def tile_attend_maplace_outside_blend_kernel(
         w_codes = sbt([P, Q], U32, "w_codes")
         w_scales = sbt([P, Q], U8, "w_scales")
         nc.vector.quantize_mx(out=w_codes[:].bitcast(X4), scales=w_scales[:], in_=w_grp[:].rearrange("p q t -> p (q t)"))
-        head_codes = sbt([P, 3, P], U32, "head_codes")
-        v_q = [quantise_values(0, grp0[:], head_codes[:, 0, :]), quantise_values(1, grp1[:], head_codes[:, 1, :])]
         picked3 = sbt([P, I], BF16, "v_picked3", "k0_then")
         gather_values(3, picked3, "vector", 0, HALF)
         gather_values(3, picked3, "scalar", HALF, HALF)
-        grp2 = sbt([P, P, PACK], BF16, "v_grp2", "v_win3_then")
+        head_codes = last.tile([P, 3, P], U32, name="head_codes", align_bytes=64, offset=0)
+        grp2 = last.tile([P, P, PACK], BF16, name="v_grp2", align_bytes=64, offset=T)
+        v_q = [quantise_values(0, grp0[:], head_codes[:, 0, :]), quantise_values(1, grp1[:], head_codes[:, 1, :])]
         turn_values(2, picked2, grp2[:])
         grp3 = sbt([P, P, PACK], BF16, "v_grp3")
         turn_values(3, picked3, grp3[:])

@@ -57,10 +57,10 @@ def tile_attend_maplace_outside_blend_kernel(
         scale_rows = keys_scales[0].bitcast(I32).rearrange("(quad r) c -> r quad c", r=4)
         for r in range(4):
             nc.sync.dma_start(out=scale_win[r:P:32, :].bitcast(I32), in_=scale_rows[r])
+        nc.sync.dma_start(out=q_raw[1][:], in_=query2.rearrange("(p t) q -> p t q", t=PACK))
         key_words = keys_words[0].rearrange("p n t -> p (n t)").bitcast(I32)
         nc.sync.dma_start(out=word_win[:, : T // 2], in_=key_words[:, : T // 2])
         nc.sync.dma_start(out=y_win[0:1, :T], in_=ymark[0:1, :])
-        nc.sync.dma_start(out=q_raw[1][:], in_=query2.rearrange("(p t) q -> p t q", t=PACK))
         nc.sync.dma_start(out=x_win[0:1, :T], in_=xmark[0:1, :])
         nc.sync.dma_start(out=word_win[:, T // 2 :], in_=key_words[:, T // 2 :])
         v_win = [sbt([P, T], F32, "v_win%d" % b, "v_win%d_then" % b) for b in range(3)]
@@ -93,10 +93,6 @@ def tile_attend_maplace_outside_blend_kernel(
         q_scales = sbt([P, 2 * Q], U8, "q_scales")
         k_scales = sbt([P, I], U8, "k_scales")
         nc.vector.tensor_copy(k_scales[:], listed(scale_win[:], 0, I))
-        y_picked = sbt([P, I], F32, "y_picked")
-        x_picked = sbt([P, I], F32, "x_picked")
-        nc.vector.tensor_copy(y_picked[:], listed(y_win[:], 0, I))
-        nc.scalar.activation(x_picked[:], listed(x_win[:], 0, I), ACT.Copy)
         nc.vector.tensor_copy(
             out=q_grp[:, 1].rearrange("p (c i) t -> p c t i", i=4),
             in_=q_raw[1][:].rearrange("p t (c i) -> p c t i", i=4),
@@ -104,6 +100,10 @@ def tile_attend_maplace_outside_blend_kernel(
         nc.vector.quantize_mx(
             out=q_codes[:].bitcast(X4), scales=q_scales[:], in_=q_grp[:].rearrange("p c q t -> p (c q t)")
         )
+        y_picked = sbt([P, I], F32, "y_picked")
+        x_picked = sbt([P, I], F32, "x_picked")
+        nc.vector.tensor_copy(y_picked[:], listed(y_win[:], 0, I))
+        nc.scalar.activation(x_picked[:], listed(x_win[:], 0, I), ACT.Copy)
 
         marks = []
         for c, picked in ((1, y_picked), (0, x_picked)):

from contextlib import ExitStack

import concourse.mybir as mybir
from concourse.masks import make_identity

D, T, I, Q, E, G = 512, 2048, 512, 128, 512, 64
P = 128
PACK = 4
HALF = I // 2
FLOPS = 2 * D * Q * I * 2 + 2 * I * Q * E

F32 = mybir.dt.float32
BF16 = mybir.dt.bfloat16
I32 = mybir.dt.int32
U32 = mybir.dt.uint32
U16 = mybir.dt.uint16
U8 = mybir.dt.uint8
X4 = mybir.dt.float8_e4m3fn_x4
ALU = mybir.AluOpType
ACT = mybir.ActivationFunctionType
AX = mybir.AxisListType


def tile_attend_maplace_outside_blend_kernel(
    tc, query, query2, keys_words, keys_scales, xmark, ymark, lam, slot_factor, vals, before, hold, offs, out
):
    nc = tc.nc
    with ExitStack() as ctx:
        lists = ctx.enter_context(tc.tile_pool(name="lists", bufs=1))
        sb = ctx.enter_context(tc.tile_pool(name="sb", bufs=1))
        last = ctx.enter_context(tc.tile_pool(name="last", bufs=1))
        ps = ctx.enter_context(tc.psum_pool(name="ps", bufs=1))

        def sbt(shape, dtype, name, tag=None):
            return sb.tile(shape, dtype, name=name, tag=tag or name, align_bytes=64)

        def bank(shape, name, number):
            return ps.tile(shape, F32, name=name, tag="bank%d" % number)

        offsets = lists.tile([P, I // 16], U16, name="offsets")
        nc.sync.dma_start(offsets[:], offs)

        def listed(window, first, count):
            return window.indirect(offsets[:, first // 16 : (first + count) // 16])

        scale_win = sbt([P, T], U8, "scale_win")
        x_win = sbt([P, T + 1], F32, "x_win", "x_win_then")
        y_win = sbt([P, T + 1], F32, "y_win")
        word_win = sbt([P, T], I32, "word_win", "words_then")
        nc.gpsimd.memset(scale_win[:].bitcast(I32), 0)
        for win, split in ((y_win, 1024), (x_win, 768)):
            nc.gpsimd.memset(win[:, :split], 0.0)
            nc.vector.memset(win[:, split:], 0.0)

        q_raw = [sbt([P, PACK, Q], F32, "q_raw%d" % c) for c in range(2)]
        nc.sync.dma_start(out=q_raw[0][:], in_=query.rearrange("(p t) q -> p t q", t=PACK))
        scale_rows = keys_scales[0].bitcast(I32).rearrange("(quad r) c -> r quad c", r=4)
        for r in range(4):
            nc.sync.dma_start(out=scale_win[r:P:32, :].bitcast(I32), in_=scale_rows[r])
        nc.sync.dma_start(out=q_raw[1][:], in_=query2.rearrange("(p t) q -> p t q", t=PACK))
        key_words = keys_words[0].rearrange("p n t -> p (n t)").bitcast(I32)
        nc.sync.dma_start(out=word_win[:, : T // 2], in_=key_words[:, : T // 2])
        nc.sync.dma_start(out=y_win[0:1, :T], in_=ymark[0:1, :])
        nc.sync.dma_start(out=x_win[0:1, :T], in_=xmark[0:1, :])
        nc.sync.dma_start(out=word_win[:, T // 2 :], in_=key_words[:, T // 2 :])
        v_win = [sbt([P, T], F32, "v_win%d" % b, "v_win%d_then" % b) for b in range(3)]
        v_win.append(last.tile([P, T], F32, name="v_win3", align_bytes=64, offset=0))
        lam_col = sbt([P, 1], F32, "lam_col")
        hold_col = sbt([P, 1], F32, "hold_col")
        os_col = sbt([P, PACK], F32, "os_col")
        before_sb = sbt([P, E], F32, "before_sb")
        riders = (
            [(lam_col, lam)],
            [(os_col, slot_factor.rearrange("o (p t) -> p (o t)", t=PACK))],
            [],
            [(hold_col, hold), (before_sb, before)],
        )
        for b, followers in enumerate(riders):
            nc.sync.dma_start(out=v_win[b][:], in_=vals[b * P : (b + 1) * P, :])
            for dst, src in followers:
                nc.sync.dma_start(out=dst[:], in_=src)

        ident = sbt([P, P], F32, "ident")
        make_identity(nc, ident[:])
        neg_lam = sbt([P, 1], F32, "neg_lam", "lam_then_values")
        keep_new = sbt([P, 1], F32, "keep_new")
        nc.gpsimd.tensor_scalar(neg_lam[:], lam_col[:], -1.0, 0.0, ALU.mult, ALU.add)
        nc.gpsimd.tensor_scalar(keep_new[:], hold_col[:], -1.0, 1.0, ALU.mult, ALU.add)

        q_grp = sbt([P, 2, Q, PACK], BF16, "q_grp")
        nc.scalar.activation(q_grp[:, 0], q_raw[0][:].rearrange("p t q -> p q t"), ACT.Copy)
        q_codes = sbt([P, 2 * Q], U32, "q_codes")
        q_scales = sbt([P, 2 * Q], U8, "q_scales")
        k_scales = sbt([P, I], U8, "k_scales")
        nc.vector.tensor_copy(k_scales[:], listed(scale_win[:], 0, I))
        nc.vector.tensor_copy(
            out=q_grp[:, 1].rearrange("p (c i) t -> p c t i", i=4),
            in_=q_raw[1][:].rearrange("p t (c i) -> p c t i", i=4),
        )
        nc.vector.quantize_mx(
            out=q_codes[:].bitcast(X4), scales=q_scales[:], in_=q_grp[:].rearrange("p c q t -> p (c q t)")
        )
        y_picked = sbt([P, I], F32, "y_picked")
        x_picked = sbt([P, I], F32, "x_picked")
        nc.vector.tensor_copy(y_picked[:], listed(y_win[:], 0, I))
        nc.scalar.activation(x_picked[:], listed(x_win[:], 0, I), ACT.Copy)

        marks = []
        for c, picked in ((1, y_picked), (0, x_picked)):
            turned = bank([P, 4, P], "mark_bank%d" % c, c)
            for j in range(4):
                nc.tensor.transpose(turned[:, j, :], picked[:, j * P : (j + 1) * P], ident[:])
            cols = sbt([P, 4, 1], F32, "mark_cols%d" % c, "x_win_then" if c == 1 else None)
            nc.scalar.copy(cols[:], turned[:, :, 0:1])
            marks.insert(0, cols)

        k_words = sbt([P, I], U32, "k_words")
        for h in range(2):
            nc.vector.tensor_copy(k_words[:, h * HALF : (h + 1) * HALF], listed(word_win[:].bitcast(U32), h * HALF, HALF))

        squares = []
        for j in range(4):
            point = bank([P, 2, Q], "point%d" % j, 2 + j)
            nc.tensor.matmul_mx(
                out=point[:].rearrange("s c q -> s (c q)"),
                lhsT=k_words[:, j * P : (j + 1) * P].bitcast(X4),
                lhsT_scale=k_scales[:, j * P : (j + 1) * P],
                rhs=q_codes[:].bitcast(X4),
                rhs_scale=q_scales[:],
                start=True,
                stop=True,
            )
            square = sbt([P, 2, Q], F32, "square%d" % j)
            for c in range(2):
                nc.scalar.activation(square[:, c, :], point[:, c, :], ACT.Square, bias=marks[c][:, j, :], scale=-1.0)
            squares.append(square)

        def gather_values(b, picked, engine, first, count):
            src = listed(v_win[b][:], first, count)
            if engine == "vector":
                nc.vector.tensor_copy(picked[:, first : first + count], src)
            else:
                nc.scalar.activation(picked[:, first : first + count], src, ACT.Copy)

        picked0 = sbt([P, I], BF16, "v_picked0", "words_then")
        gather_values(0, picked0, "vector", 0, I)

        p_t = sbt([P, PACK, P], F32, "p_t")
        z = [sbt([P, 1], F32, "z%d" % h, "z%d_then" % h) for h in range(2)]
        neg_pg = sbt([P, G], F32, "neg_pg", "v_win0_then")
        for h in range(2):
            dist = bank([P, 2, P], "dist%d" % h, 6 + h)
            for j in range(2):
                for c in range(2):
                    nc.tensor.matmul(
                        dist[:, j, :], squares[2 * h + j][:, c, :], ident[:], is_transpose=True,
                        start=(c == 0), stop=(c == 1),
                    )
            p_half = p_t[:, :, h * P // 2 : (h + 1) * P // 2]
            nc.scalar.activation(
                p_half, dist[:].rearrange("q j m -> q (j m)").rearrange("q (s t) -> q t s", t=PACK),
                ACT.Exp, scale=neg_lam[:], accum_out=z[h][:],
            )
            nc.vector.tensor_reduce(
                neg_pg[:, h * G // 2 : (h + 1) * G // 2], p_half.rearrange("q t (g r) -> q g t r", r=2), AX.XY, ALU.add,
                negate=True,
            )

        def turn_values(b, picked, grp):
            words = picked[:].bitcast(F32)
            turned = bank([P, 2, P], "v_bank%d" % b, (7, 6, 4, 2)[b])
            for u in range(2):
                nc.tensor.transpose(turned[:, u, :], words[:, u : I // 2 : 2], ident[:])
            nc.scalar.copy(grp.bitcast(F32), turned[:].rearrange("p u e -> p e u"))

        def quantise_values(b, grp, codes):
            scales = sbt([P, P], U8, "v_scales%d" % b)
            nc.vector.quantize_mx(out=codes.bitcast(X4), scales=scales[:], in_=grp.rearrange("p e t -> p (e t)"))
            return codes, scales

        p_bank = bank([P, PACK, Q], "p_bank", 4)
        for t in range(PACK):
            nc.tensor.transpose(p_bank[:, t, :], p_t[:, t, :], ident[:])

        grp0 = sbt([P, P, PACK], BF16, "v_grp0")
        turn_values(0, picked0, grp0[:])
        picked1 = sbt([P, I], BF16, "v_picked1", "lam_then_values")
        gather_values(1, picked1, "scalar", 0, I)

        rest = sbt([P, G], F32, "rest")
        nc.vector.tensor_scalar(rest[:], neg_pg[:], z[0][:], z[1][:], ALU.add, ALU.add)
        k0 = sbt([P, G, 1], F32, "k0", "k0_then")
        nc.vector.reciprocal(k0[:, :, 0], rest[:])
        k2 = sbt([P, G, 2], F32, "k2")
        nc.vector.tensor_copy(k2[:], k0[:].broadcast_to([P, G, 2]))
        k_bank = bank([P, Q], "k_bank", 5)
        nc.tensor.transpose(k_bank[:], k2[:].rearrange("q g r -> q (g r)"), ident[:])
        po = sbt([P, Q, PACK], F32, "po")
        nc.vector.tensor_tensor(
            po[:], p_bank[:].rearrange("s t q -> s q t"), os_col[:].unsqueeze(1).broadcast_to([P, Q, PACK]), ALU.mult
        )
        picked2 = sbt([P, I], BF16, "v_picked2", "z1_then")
        gather_values(2, picked2, "scalar", 0, I)
        grp1 = sbt([P, P, PACK], BF16, "v_grp1", "v_win2_then")
        turn_values(1, picked1, grp1[:])
        w_grp = sbt([P, Q, PACK], BF16, "w_grp")
        nc.vector.tensor_tensor(w_grp[:], k_bank[:].unsqueeze(2).broadcast_to([P, Q, PACK]), po[:], ALU.mult)
        w_codes = sbt([P, Q], U32, "w_codes")
        w_scales = sbt([P, Q], U8, "w_scales")
        nc.vector.quantize_mx(out=w_codes[:].bitcast(X4), scales=w_scales[:], in_=w_grp[:].rearrange("p q t -> p (q t)"))
        picked3 = sbt([P, I], BF16, "v_picked3", "k0_then")
        gather_values(3, picked3, "vector", 0, HALF)
        gather_values(3, picked3, "scalar", HALF, HALF)
        head_codes = last.tile([P, 3, P], U32, name="head_codes", align_bytes=64, offset=0)
        grp2 = last.tile([P, P, PACK], BF16, name="v_grp2", align_bytes=64, offset=T)
        v_q = [quantise_values(0, grp0[:], head_codes[:, 0, :]), quantise_values(1, grp1[:], head_codes[:, 1, :])]
        turn_values(2, picked2, grp2[:])
        grp3 = sbt([P, P, PACK], BF16, "v_grp3")
        turn_values(3, picked3, grp3[:])
        v_q.append(quantise_values(2, grp2[:], head_codes[:, 2, :]))

        def product(dst, b):
            nc.tensor.matmul_mx(
                out=dst, lhsT=w_codes[:].bitcast(X4), lhsT_scale=w_scales[:],
                rhs=v_q[b][0].bitcast(X4), rhs_scale=v_q[b][1][:], start=True, stop=True,
            )

        o_head = bank([P, 3, P], "o_head", 4)
        for b in range(3):
            product(o_head[:, b, :], b)

        kept = sbt([P, E], F32, "kept")
        nc.gpsimd.tensor_scalar(kept[:], before_sb[:], hold_col[:], 0.0, ALU.mult, ALU.add)
        y_head = sbt([P, 3 * P], F32, "y_head")
        nc.vector.scalar_tensor_tensor(
            y_head[:], o_head[:].rearrange("q b e -> q (b e)"), keep_new[:], kept[:, : 3 * P], ALU.mult, ALU.add
        )
        nc.sync.dma_start(out=out[:, : 3 * P], in_=y_head[:])

        tail_codes = sbt([P, P], U32, "tail_codes")
        v_q.append(quantise_values(3, grp3[:], tail_codes[:]))
        o_tail = bank([P, P], "o_tail", 1)
        product(o_tail[:], 3)
        y_tail = sbt([P, P], F32, "y_tail")
        nc.vector.scalar_tensor_tensor(y_tail[:], o_tail[:], keep_new[:], kept[:, 3 * P :], ALU.mult, ALU.add)
        nc.sync.dma_start(out=out[:, 3 * P :], in_=y_tail[:])
